import numpy as np
import ml_dtypes


def mxq(x, axis, fmt="e4m3"):
    dtype, down = {"e4m3": (ml_dtypes.float8_e4m3fn, 7), "e5m2": (ml_dtypes.float8_e5m2, 14)}[fmt]
    v = np.moveaxis(np.asarray(x, np.float32).astype(ml_dtypes.bfloat16).astype(np.float64), axis, -1)
    blocks = v.reshape(v.shape[:-1] + (-1, 32))
    amax = np.abs(blocks).max(-1, keepdims=True)
    byte = np.maximum(np.where(amax > 0, np.frexp(amax)[1] - 1 + 127, 0) - down, 1)
    scale = np.exp2(byte - 127.0)
    codes = (blocks / scale).astype(np.float32).astype(dtype).astype(np.float64)
    return np.moveaxis((codes * scale).reshape(v.shape), -1, axis)


WIDE = False


def mx_kscale(k):
    if not WIDE:
        return np.ones(k)
    levels = np.array([10, -10, 5, -5, 0])
    if k % 512:
        return np.exp2(np.random.permutation(np.resize(levels, k // 32))).repeat(32)
    a = np.empty((k // 512, 16))
    for p in range(k // 512):
        a[p, :8] = np.random.permutation(np.resize(levels, 8))
        for g in range(8):
            far = levels[np.abs(levels - a[p, g]) >= 10]
            a[p, g + 8] = far[np.random.randint(len(far))]
    return np.exp2(a.ravel()).repeat(32)


def f64(x):
    return np.asarray(x).astype(np.float64)


def striped(idx):
    return np.tile(idx.reshape(-1, 16).T, (8, 1)).astype(np.uint16)


def unstriped(offs):
    return offs[:16].T.reshape(-1).astype(np.int64)


def pack_weight(w):
    k, n = w.shape
    w = f64(np.asarray(w, np.float32).astype(ml_dtypes.bfloat16)).reshape(k // 32, 32, n)
    amax = np.abs(w).max(1)
    byte = np.clip(np.where(amax > 0, np.frexp(amax)[1] - 1 + 127 - 7, 1), 1, 254)
    scaled = (w * np.exp2(127.0 - byte)[:, None, :]).reshape(k, n).astype(np.float32)
    words = np.ascontiguousarray(scaled.reshape(k // 512, 128, 4, n).transpose(0, 1, 3, 2)).astype(ml_dtypes.float8_e4m3fn).view(np.uint8)
    return words, np.ascontiguousarray(byte.astype(np.uint8).reshape(k // 512, 16, n))


def unpack_weight(words, scales):
    g, p, n, _ = words.shape
    vals = np.ascontiguousarray(words).view(ml_dtypes.float8_e4m3fn).astype(np.float64) * np.repeat(np.exp2(scales.astype(np.float64) - 127.0), 8, axis=1)[..., None]
    return vals.transpose(0, 1, 3, 2).reshape(g * 512, n)


E2M1 = np.array([0.0, 0.5, 1.0, 1.5, 2.0, 3.0, 4.0, 6.0, -0.0, -0.5, -1.0, -1.5, -2.0, -3.0, -4.0, -6.0])


def pack_fp4(w):
    k, n = w.shape
    w = f64(np.asarray(w, np.float32).astype(ml_dtypes.bfloat16)).reshape(k // 32, 32, n)
    amax = np.abs(w).max(1)
    mant, ex = np.frexp(amax / 6.0)
    byte = np.clip(np.where(amax > 0, np.where(mant > 0.5, ex, ex - 1) + 127, 1), 1, 254)
    scaled = (w * np.exp2(127.0 - byte)[:, None, :]).reshape(k, n).astype(np.float32)
    c = np.ascontiguousarray(scaled.reshape(k // 512, 128, 4, n).transpose(0, 1, 3, 2)).astype(ml_dtypes.float4_e2m1fn).view(np.uint8) & 0xF
    words = (c[..., 0::2] | (c[..., 1::2] << 4)).reshape(k // 512, 128, 2 * n)
    return np.ascontiguousarray(words), np.ascontiguousarray(byte.astype(np.uint8).reshape(k // 512, 16, n))


def unpack_fp4(words, scales):
    g, _, n = scales.shape
    words = np.ascontiguousarray(words).reshape(g, 128, n, 2)
    nib = np.empty((g, 128, n, 4), np.uint8)
    nib[..., 0::2] = words & 0xF
    nib[..., 1::2] = words >> 4
    vals = E2M1[nib] * np.repeat(np.exp2(scales.astype(np.float64) - 127.0), 8, axis=1)[..., None]
    return vals.transpose(0, 1, 3, 2).reshape(g * 512, n)


K, T, S, N, H = 1024, 1024, 512, 256, 512


def setup_inputs():
    n = np.random.standard_normal
    s = mx_kscale(K)[:, None]
    u = mx_kscale(H)
    packed_xT = pack_weight(n((K, T)) * s)
    packed_w1 = pack_fp4(n((K, H)) / np.sqrt(K) / s)
    packed_w2 = pack_fp4(n((K, H)) / np.sqrt(K) / s)
    packed_w3 = pack_fp4(n((H, N)) / np.sqrt(H) / u[:, None])
    return {
        "x_words": packed_xT[0],
        "x_scales": packed_xT[1],
        "w1_words": packed_w1[0],
        "w1_scales": packed_w1[1],
        "w2_words": packed_w2[0],
        "w2_scales": packed_w2[1],
        "u1": (n((H, S))).astype(np.float32),
        "u2": (n((H, S))).astype(np.float32),
        "thr": (np.random.uniform(0.3, 1.0, (H, S))).astype(np.float32),
        "unit": (np.random.uniform(0.6, 1.4, (H, 1)) * u[:, None]).astype(np.float32),
        "w3_words": packed_w3[0],
        "w3_scales": packed_w3[1],
        "offs": striped(np.random.permutation(T)[:S]),
        "mod": striped(np.random.permutation(S)),
    }


def reference(x_words, x_scales, w1_words, w1_scales, w2_words, w2_scales, u1, u2, thr, unit, w3_words, w3_scales, offs, mod):
    xq = unpack_weight(x_words, x_scales)[:, unstriped(offs)]
    la = unpack_fp4(w1_words, w1_scales).T @ xq
    lb = unpack_fp4(w2_words, w2_scales).T @ xq
    alg = la * f64(u1) + lb * f64(u2)
    lm = la[:, unstriped(mod)]
    grad = (la) ** 2 + (lb) ** 2 + 0.5 * ((lm) ** 2) + 0.3
    samp = ((alg) ** 2) / grad
    gm = f64(thr) / (samp + f64(thr))
    wm = gm[:, unstriped(mod)]
    hid = f64(unit) * ((gm) ** 2 - (0.5 * wm))
    return unpack_fp4(w3_words, w3_scales).T @ mxq(hid, 0, "e4m3")

@@ -1,0 +1,260 @@
+from contextlib import ExitStack
+
+import concourse.mybir as mybir
+from concourse.masks import make_identity
+
+K, T, S, N, H = 1024, 1024, 512, 256, 512
+FLOPS = 2 * (2 * K * H * S + H * N * S)
+
+F32 = mybir.dt.float32
+BF16 = mybir.dt.bfloat16
+I32 = mybir.dt.int32
+U32 = mybir.dt.uint32
+U16 = mybir.dt.uint16
+U8 = mybir.dt.uint8
+FP8X4 = mybir.dt.float8_e4m3fn_x4
+FP4X4 = mybir.dt.float4_e2m1fn_x4
+ACT = mybir.ActivationFunctionType
+ALU = mybir.AluOpType
+
+P = 128
+PACK = 4
+PASSES = K // (P * PACK)
+QUADS = 4
+BLOCKS = S // P
+FRONT = 8
+HM_ON_V = ()
+ALG_ON_PE = ()
+ORDER = (0, 1, 2, 3, 4)
+LAG = (0, 0, 0, 0, 4)
+CHUNKS = (128, 128, 128, 128)
+WORK = 4
+DEAL_V = ()
+
+
+def tile_picked_ysampso_pair_p_kernel(
+    tc, x_words, x_scales, w1_words, w1_scales, w2_words, w2_scales, u1, u2, thr, unit, w3_words, w3_scales, offs, mod, out
+):
+    nc = tc.nc
+    with ExitStack() as ctx:
+        keep = ctx.enter_context(tc.tile_pool(name="keep", bufs=1))
+        work = ctx.enter_context(tc.tile_pool(name="work", bufs=WORK))
+        psum = ctx.enter_context(tc.psum_pool(name="psum", bufs=1))
+
+        offs_sb = keep.tile([P, S // 16], U16, name="offs_sb")
+        mod_sb = keep.tile([P, S // 16], U16, name="mod_sb")
+        xs_raw = keep.tile([P, PASSES, T], U8, name="xs_raw", align_bytes=64)
+        ws_raw = [keep.tile([P, PASSES, H], U8, name=f"ws_raw{n}", align_bytes=64) for n in range(2)]
+        w3s = keep.tile([P, 1, N], U8, name="w3s", align_bytes=64)
+        ww_raw = [keep.tile([P, PASSES, 2 * H], U8, name=f"ww_raw{n}", align_bytes=64) for n in range(2)]
+        w3w = keep.tile([P, 2 * N], U8, name="w3w", align_bytes=64)
+        xw_raw = [keep.tile([P, T], U32, name=f"xw_raw{o}", align_bytes=64) for o in range(PASSES)]
+        ident = keep.tile([P, P], F32, name="ident")
+        unit_sb = keep.tile([P, PACK], F32, name="unit_sb")
+
+        nc.gpsimd.memset(xs_raw[:].bitcast(I32), 0)
+        for n in range(2):
+            nc.vector.memset(ws_raw[n][:].bitcast(I32), 0)
+        nc.vector.memset(w3s[:].bitcast(I32), 0)
+        if ALG_ON_PE:
+            make_identity(nc, ident[:])
+
+        def load_scale_rows(dst, src, queue=nc.sync):
+            for q in range(QUADS):
+                queue.dma_start(
+                    out=dst[32 * q : 32 * q + 4].bitcast(I32),
+                    in_=src[:, 4 * q : 4 * q + 4, :].rearrange("o r c -> r o c").bitcast(I32),
+                )
+
+        def load_words(dst, src):
+            nc.sync.dma_start(out=dst[:].bitcast(I32), in_=src.rearrange("o p c -> p o c").bitcast(I32))
+
+        def load_x(o):
+            nc.sync.dma_start(out=xw_raw[o][:].bitcast(I32), in_=x_words[o].rearrange("p n t -> p (n t)").bitcast(I32))
+
+        u1_sb, u2_sb, thr_sb = {}, {}, {}
+
+        def load_rows(name, src, dst, t):
+            dst[t] = keep.tile([P, S], F32, name=f"{name}_{t}")
+            nc.sync.dma_start(out=dst[t][:], in_=src.rearrange("(p t) j -> t p j", t=PACK)[t])
+
+        load_words(ww_raw[0], w1_words)
+        nc.sync.dma_start(offs_sb[:], offs)
+        load_scale_rows(xs_raw[:], x_scales)
+        load_x(0)
+        load_words(ww_raw[1], w2_words)
+        load_scale_rows(ws_raw[0][:], w1_scales)
+        load_x(1)
+        load_scale_rows(ws_raw[1][:], w2_scales)
+        load_rows("u1", u1, u1_sb, 0)
+        load_rows("u2", u2, u2_sb, 0)
+        nc.sync.dma_start(mod_sb[:], mod)
+        load_rows("thr", thr, thr_sb, 0)
+        nc.sync.dma_start(out=unit_sb[:], in_=unit.rearrange("(p t) o -> p (t o)", t=PACK))
+        for t in range(PACK):
+            for name, src, dst in (("u1", u1, u1_sb), ("u2", u2, u2_sb), ("thr", thr, thr_sb)):
+                if t not in dst:
+                    load_rows(name, src, dst, t)
+        nc.sync.dma_start(out=w3w[:].bitcast(I32), in_=w3_words[0].bitcast(I32))
+        load_scale_rows(w3s[:], w3_scales)
+
+        ww, ws = {}, {}
+        for t in range(PACK):
+            for n in range(2):
+                words = keep.tile([P, PASSES, 2 * P], U8, name=f"ww{n}{t}", align_bytes=64)
+                (nc.vector if (n, t) in DEAL_V else nc.gpsimd).tensor_copy(
+                    out=words[:].rearrange("p a (m b) -> p a m b", b=2),
+                    in_=ww_raw[n][:].rearrange("p a (m t b) -> p a t m b", t=PACK, b=2)[:, :, t],
+                )
+                scales = keep.tile([P, PASSES, P], U8, name=f"ws{n}{t}", align_bytes=64)
+                nc.gpsimd.tensor_copy(out=scales[:], in_=ws_raw[n][:].rearrange("p a (m t) -> p a t m", t=PACK)[:, :, t])
+                ww[n, t] = words
+                ws[n, t] = scales
+
+        xs, xw = [], []
+        for o in range(PASSES):
+            g = keep.tile([P, S], U8, name=f"xs{o}", align_bytes=64)
+            nc.vector.tensor_copy(g[:], xs_raw[:, o, :].indirect(offs_sb[:]))
+            xs.append(g)
+        for o in range(PASSES):
+            g = keep.tile([P, S], U32, name=f"xw{o}", align_bytes=64)
+            nc.vector.tensor_copy(g[:], xw_raw[o][:].indirect(offs_sb[:]))
+            xw.append(g)
+
+        gain = keep.tile([P, PACK], F32, name="gain")
+        nc.vector.tensor_scalar(gain[:], unit_sb[:], -0.5, None, ALU.mult)
+
+        banks = {}
+
+        def products(t):
+            for n in range(2):
+                bank = psum.tile([P, S], F32, name="bank", bufs=FRONT)
+                for o in range(PASSES):
+                    nc.tensor.matmul_mx(
+                        out=bank[:],
+                        lhsT=ww[n, t][:, o, :].bitcast(FP4X4),
+                        lhsT_scale=ws[n, t][:, o, :],
+                        rhs=xw[o][:].bitcast(FP8X4),
+                        rhs_scale=xs[o][:],
+                        start=(o == 0),
+                        stop=(o == PASSES - 1),
+                    )
+                banks[n, t] = bank
+
+        odds = keep.tile([P, PACK, S], F32, name="odds")
+
+        def turn(dst, parts):
+            for b in range(0, S, P):
+                for n, part in enumerate(parts):
+                    nc.tensor.matmul(
+                        dst[:, b : b + P],
+                        part[:, b : b + P],
+                        ident[:],
+                        start=(n == 0),
+                        stop=(n == len(parts) - 1),
+                        is_transpose=True,
+                    )
+
+        state = {}
+
+        def terms(t):
+            la, lb = banks[0, t], banks[1, t]
+            win = work.tile([P, 2 * S], F32, name="win")
+            a1 = work.tile([P, S], F32, name="a1")
+            a2 = work.tile([P, S], F32, name="a2")
+            nc.scalar.activation(win[:, :S], la[:], ACT.Square, scale=0.5**0.5)
+            nc.vector.tensor_tensor(a1[:], la[:], u1_sb[t][:], ALU.mult)
+            nc.scalar.activation(win[:, S:], lb[:], ACT.Square)
+            nc.vector.tensor_tensor(a2[:], lb[:], u2_sb[t][:], ALU.mult)
+            state[t] = (win, a1, a2)
+
+        def sums(t):
+            win, a1, a2 = state[t]
+            own = work.tile([P, S], F32, name="own")
+            grad = work.tile([P, S], F32, name="grad")
+            nc.vector.scalar_tensor_tensor(own[:], win[:, :S], 2.0, win[:, S:], ALU.mult, ALU.add)
+            if t in ALG_ON_PE:
+                alg = psum.tile([P, S], F32, name="turned", bufs=8 - FRONT)
+                turn(alg, (a1, a2))
+            else:
+                alg = work.tile([P, S], F32, name="alg")
+                nc.vector.tensor_tensor(alg[:], a1[:], a2[:], ALU.add)
+            if t in HM_ON_V:
+                nc.vector.tensor_tensor(grad[:], win[:].indirect(mod_sb[:]), own[:], ALU.add)
+            else:
+                partner = work.tile([P, S], F32, name="partner")
+                nc.scalar.activation(partner[:], win[:].indirect(mod_sb[:]), ACT.Copy)
+                nc.vector.tensor_tensor(grad[:], partner[:], own[:], ALU.add)
+            state[t] = (alg, grad)
+
+        def logs(t):
+            alg, grad = state[t]
+            alg2 = work.tile([P, S], F32, name="alg2")
+            log_alg = work.tile([P, S], F32, name="log_alg")
+            log_num = work.tile([P, S], F32, name="log_num")
+            num = work.tile([P, S], F32, name="num")
+            nc.scalar.activation(alg2[:], alg[:], ACT.Square)
+            nc.scalar.activation(log_alg[:], alg2[:], ACT.Ln, bias=2.0**-60)
+            if t in ALG_ON_PE:
+                back = psum.tile([P, S], F32, name="turned", bufs=8 - FRONT)
+                turn(back, (log_alg,))
+                log_alg = back
+            nc.vector.scalar_tensor_tensor(num[:], grad[:], 0.3, thr_sb[t][:], ALU.add, ALU.mult)
+            nc.scalar.activation(log_num[:], num[:], ACT.Ln)
+            state[t] = (log_num, log_alg)
+
+        def log_odds(t):
+            log_num, log_alg = state[t]
+            nc.vector.tensor_tensor(odds[:, t, :], log_num[:], log_alg[:], ALU.subtract)
+
+        stages = (products, terms, sums, logs, log_odds)
+        for step in range(PACK + max(LAG)):
+            for depth in ORDER:
+                t = step - LAG[depth]
+                if 0 <= t < PACK:
+                    stages[depth](t)
+
+        half = S // 2
+        gm = keep.tile([P, PACK, S], F32, name="gm")
+        for c in range(2):
+            cols = slice(c * half, (c + 1) * half)
+            nc.scalar.activation(gm[:, :, cols], odds[:, :, cols], ACT.Sigmoid)
+
+        square = keep.tile([P, PACK, S], F32, name="square")
+        for c in range(2):
+            cols = slice(c * half, (c + 1) * half)
+            for t in range(PACK):
+                nc.vector.scalar_tensor_tensor(square[:, t, cols], gm[:, t, cols], unit_sb[:, t : t + 1], gm[:, t, cols], ALU.mult, ALU.mult)
+
+        start = 0
+        for width in CHUNKS:
+            cols = slice(start, start + width)
+            picks = mod_sb[:, start // 16 : (start + width) // 16]
+            start += width
+            planes = work.tile([P, PACK, width], BF16, name="planes", align_bytes=64)
+            for t in range(PACK):
+                wm = work.tile([P, width], F32, name="wm", bufs=8)
+                nc.scalar.activation(wm[:], gm[:, t, :].indirect(picks), ACT.Copy)
+                nc.vector.scalar_tensor_tensor(planes[:, t, :], wm[:], gain[:, t : t + 1], square[:, t, cols], ALU.mult, ALU.add)
+            grouped = work.tile([P, width, PACK], BF16, name="grouped", align_bytes=64)
+            codes = work.tile([P, width], U32, name="codes", align_bytes=64)
+            hscale = work.tile([P, width], U8, name="hscale", align_bytes=64)
+            nc.vector.tensor_copy(
+                out=grouped[:].rearrange("p (c i) t -> p c t i", i=4),
+                in_=planes[:].rearrange("p t (c i) -> p c t i", i=4),
+            )
+            nc.vector.quantize_mx(out=codes[:].bitcast(FP8X4), scales=hscale[:], in_=grouped[:].rearrange("p c t -> p (c t)"))
+            bank = psum.tile([P, 2, width], F32, name="bank", bufs=FRONT)
+            for m in range(N // P):
+                nc.tensor.matmul_mx(
+                    out=bank[:, m, :],
+                    lhsT=w3w[:, m * 2 * P : (m + 1) * 2 * P].bitcast(FP4X4),
+                    lhsT_scale=w3s[:, 0, m * P : (m + 1) * P],
+                    rhs=codes[:].bitcast(FP8X4),
+                    rhs_scale=hscale[:],
+                    start=True,
+                    stop=True,
+                )
+            res = work.tile([P, 2, width], F32, name="res")
+            nc.scalar.copy(res[:], bank[:])
+            nc.sync.dma_start(out=out[:, cols].rearrange("(m p) j -> p m j", p=P), in_=res[:])

@@ -20,16 +20,19 @@ ALU = mybir.AluOpType
 P = 128
 PACK = 4
 PASSES = K // (P * PACK)
-QUADS = 4
-BLOCKS = S // P
-FRONT = 8
-HM_ON_V = ()
-ALG_ON_PE = ()
-ORDER = (0, 1, 2, 3, 4)
-LAG = (0, 0, 0, 0, 4)
-CHUNKS = (128, 128, 128, 128)
-WORK = 4
-DEAL_V = ()
+QUADRANTS = 4
+FP4_BYTES = 2
+PER_COLUMN = 16
+BANKS = 8
+WORK_BUFS = PACK
+CHUNK = 128
+RUN = 4
+
+LOG_FLOOR = 2.0**-60
+
+PARTNER_ON_VECTOR = (0, 3)
+
+SUMS_LAG, LOGS_LAG = 1, 3
 
 
 def tile_picked_ysampso_pair_p_kernel(
@@ -38,16 +41,16 @@ def tile_picked_ysampso_pair_p_kernel(
     nc = tc.nc
     with ExitStack() as ctx:
         keep = ctx.enter_context(tc.tile_pool(name="keep", bufs=1))
-        work = ctx.enter_context(tc.tile_pool(name="work", bufs=WORK))
-        psum = ctx.enter_context(tc.psum_pool(name="psum", bufs=1))
+        work = ctx.enter_context(tc.tile_pool(name="work", bufs=WORK_BUFS))
+        psum = ctx.enter_context(tc.psum_pool(name="psum", bufs=BANKS))
 
-        offs_sb = keep.tile([P, S // 16], U16, name="offs_sb")
-        mod_sb = keep.tile([P, S // 16], U16, name="mod_sb")
+        offs_sb = keep.tile([P, S // PER_COLUMN], U16, name="offs_sb")
+        mod_sb = keep.tile([P, S // PER_COLUMN], U16, name="mod_sb")
         xs_raw = keep.tile([P, PASSES, T], U8, name="xs_raw", align_bytes=64)
         ws_raw = [keep.tile([P, PASSES, H], U8, name=f"ws_raw{n}", align_bytes=64) for n in range(2)]
         w3s = keep.tile([P, 1, N], U8, name="w3s", align_bytes=64)
-        ww_raw = [keep.tile([P, PASSES, 2 * H], U8, name=f"ww_raw{n}", align_bytes=64) for n in range(2)]
-        w3w = keep.tile([P, 2 * N], U8, name="w3w", align_bytes=64)
+        ww_raw = [keep.tile([P, PASSES, FP4_BYTES * H], U8, name=f"ww_raw{n}", align_bytes=64) for n in range(2)]
+        w3w = keep.tile([P, FP4_BYTES * N], U8, name="w3w", align_bytes=64)
         xw_raw = [keep.tile([P, T], U32, name=f"xw_raw{o}", align_bytes=64) for o in range(PASSES)]
         ident = keep.tile([P, P], F32, name="ident")
         unit_sb = keep.tile([P, PACK], F32, name="unit_sb")
@@ -56,205 +59,207 @@ def tile_picked_ysampso_pair_p_kernel(
         for n in range(2):
             nc.vector.memset(ws_raw[n][:].bitcast(I32), 0)
         nc.vector.memset(w3s[:].bitcast(I32), 0)
-        if ALG_ON_PE:
-            make_identity(nc, ident[:])
+        make_identity(nc, ident[:])
 
-        def load_scale_rows(dst, src, queue=nc.sync):
-            for q in range(QUADS):
-                queue.dma_start(
+        warm = keep.tile([P, 2], F32, name="warm")
+        nc.vector.memset(warm[:, 0:1], 1.0)
+        nc.scalar.activation(warm[:, 1:2], warm[:, 0:1], ACT.Ln)
+
+        def load_scale_rows(dst, src):
+            for q in range(QUADRANTS):
+                nc.sync.dma_start(
                     out=dst[32 * q : 32 * q + 4].bitcast(I32),
                     in_=src[:, 4 * q : 4 * q + 4, :].rearrange("o r c -> r o c").bitcast(I32),
                 )
 
-        def load_words(dst, src):
-            nc.sync.dma_start(out=dst[:].bitcast(I32), in_=src.rearrange("o p c -> p o c").bitcast(I32))
+        def load_w_words(n, src):
+            nc.sync.dma_start(out=ww_raw[n][:].bitcast(I32), in_=src.rearrange("o p c -> p o c").bitcast(I32))
 
-        def load_x(o):
+        def load_x_words(o):
             nc.sync.dma_start(out=xw_raw[o][:].bitcast(I32), in_=x_words[o].rearrange("p n t -> p (n t)").bitcast(I32))
 
-        u1_sb, u2_sb, thr_sb = {}, {}, {}
+        rows = {}
 
-        def load_rows(name, src, dst, t):
-            dst[t] = keep.tile([P, S], F32, name=f"{name}_{t}")
-            nc.sync.dma_start(out=dst[t][:], in_=src.rearrange("(p t) j -> t p j", t=PACK)[t])
+        def load_rows(name, src, t):
+            rows[name, t] = keep.tile([P, S], F32, name=f"{name}_{t}")
+            nc.sync.dma_start(out=rows[name, t][:], in_=src.rearrange("(p t) j -> t p j", t=PACK)[t])
 
-        load_words(ww_raw[0], w1_words)
+        load_w_words(0, w1_words)
         nc.sync.dma_start(offs_sb[:], offs)
         load_scale_rows(xs_raw[:], x_scales)
-        load_x(0)
-        load_words(ww_raw[1], w2_words)
+        load_x_words(0)
+        load_w_words(1, w2_words)
         load_scale_rows(ws_raw[0][:], w1_scales)
-        load_x(1)
+        load_x_words(1)
         load_scale_rows(ws_raw[1][:], w2_scales)
-        load_rows("u1", u1, u1_sb, 0)
-        load_rows("u2", u2, u2_sb, 0)
+        load_rows("u1", u1, 0)
+        load_rows("u2", u2, 0)
         nc.sync.dma_start(mod_sb[:], mod)
-        load_rows("thr", thr, thr_sb, 0)
+        load_rows("thr", thr, 0)
         nc.sync.dma_start(out=unit_sb[:], in_=unit.rearrange("(p t) o -> p (t o)", t=PACK))
-        for t in range(PACK):
-            for name, src, dst in (("u1", u1, u1_sb), ("u2", u2, u2_sb), ("thr", thr, thr_sb)):
-                if t not in dst:
-                    load_rows(name, src, dst, t)
+        for t in range(1, PACK):
+            load_rows("u1", u1, t)
+            load_rows("u2", u2, t)
+            load_rows("thr", thr, t)
         nc.sync.dma_start(out=w3w[:].bitcast(I32), in_=w3_words[0].bitcast(I32))
         load_scale_rows(w3s[:], w3_scales)
 
         ww, ws = {}, {}
-        for t in range(PACK):
-            for n in range(2):
-                words = keep.tile([P, PASSES, 2 * P], U8, name=f"ww{n}{t}", align_bytes=64)
-                (nc.vector if (n, t) in DEAL_V else nc.gpsimd).tensor_copy(
-                    out=words[:].rearrange("p a (m b) -> p a m b", b=2),
-                    in_=ww_raw[n][:].rearrange("p a (m t b) -> p a t m b", t=PACK, b=2)[:, :, t],
-                )
-                scales = keep.tile([P, PASSES, P], U8, name=f"ws{n}{t}", align_bytes=64)
-                nc.gpsimd.tensor_copy(out=scales[:], in_=ws_raw[n][:].rearrange("p a (m t) -> p a t m", t=PACK)[:, :, t])
-                ww[n, t] = words
-                ws[n, t] = scales
+
+        def deal_words(engine, n, first, count, tag):
+            words = keep.tile([P, PASSES, count, FP4_BYTES * P], U8, name=f"ww{n}_{first}", tag=tag, align_bytes=64)
+            engine.tensor_copy(
+                out=words[:].rearrange("p o t (m b) -> p o t m b", b=FP4_BYTES),
+                in_=ww_raw[n][:].rearrange("p o (m t b) -> p o t m b", t=PACK, b=FP4_BYTES)[:, :, first : first + count],
+            )
+            for t in range(count):
+                ww[n, first + t] = words[:, :, t, :]
+
+        def deal_scales(n):
+            ws[n] = keep.tile([P, PASSES, PACK, P], U8, name=f"ws{n}", align_bytes=64)
+            nc.gpsimd.tensor_copy(out=ws[n][:], in_=ws_raw[n][:].rearrange("p o (m t) -> p o t m", t=PACK))
+
+        deal_words(nc.gpsimd, 0, 0, PACK, "ww0")
+        deal_scales(0)
+        deal_words(nc.gpsimd, 1, 0, 1, "ws_raw0")
+        deal_scales(1)
 
         xs, xw = [], []
         for o in range(PASSES):
-            g = keep.tile([P, S], U8, name=f"xs{o}", align_bytes=64)
-            nc.vector.tensor_copy(g[:], xs_raw[:, o, :].indirect(offs_sb[:]))
-            xs.append(g)
+            picked_scales = keep.tile([P, S], U8, name=f"xs{o}", align_bytes=64)
+            nc.vector.tensor_copy(picked_scales[:], xs_raw[:, o, :].indirect(offs_sb[:]))
+            xs.append(picked_scales)
         for o in range(PASSES):
-            g = keep.tile([P, S], U32, name=f"xw{o}", align_bytes=64)
-            nc.vector.tensor_copy(g[:], xw_raw[o][:].indirect(offs_sb[:]))
-            xw.append(g)
+            picked_words = keep.tile([P, S], U32, name=f"xw{o}", align_bytes=64)
+            nc.vector.tensor_copy(picked_words[:], xw_raw[o][:].indirect(offs_sb[:]))
+            xw.append(picked_words)
 
-        gain = keep.tile([P, PACK], F32, name="gain")
-        nc.vector.tensor_scalar(gain[:], unit_sb[:], -0.5, None, ALU.mult)
+        deal_words(nc.vector, 1, 1, PACK - 1, f"xw_raw{PASSES - 1}")
 
-        banks = {}
+        half_unit = keep.tile([P, PACK], F32, name="half_unit")
+        nc.vector.tensor_scalar(half_unit[:], unit_sb[:], -0.5, None, ALU.mult)
 
-        def products(t):
+        products = {}
+        for t in range(PACK):
             for n in range(2):
-                bank = psum.tile([P, S], F32, name="bank", bufs=FRONT)
+                products[n, t] = psum.tile([P, S], F32, name="product", tag="bank")
                 for o in range(PASSES):
                     nc.tensor.matmul_mx(
-                        out=bank[:],
+                        out=products[n, t][:],
                         lhsT=ww[n, t][:, o, :].bitcast(FP4X4),
-                        lhsT_scale=ws[n, t][:, o, :],
+                        lhsT_scale=ws[n][:, o, t, :],
                         rhs=xw[o][:].bitcast(FP8X4),
                         rhs_scale=xs[o][:],
                         start=(o == 0),
                         stop=(o == PASSES - 1),
                     )
-                banks[n, t] = bank
 
-        odds = keep.tile([P, PACK, S], F32, name="odds")
-
-        def turn(dst, parts):
+        def transpose_and_add(parts):
+            bank = psum.tile([P, S], F32, name="turned", tag="bank")
             for b in range(0, S, P):
                 for n, part in enumerate(parts):
                     nc.tensor.matmul(
-                        dst[:, b : b + P],
+                        bank[:, b : b + P],
                         part[:, b : b + P],
                         ident[:],
                         start=(n == 0),
                         stop=(n == len(parts) - 1),
                         is_transpose=True,
                     )
+            return bank
 
-        state = {}
+        def first_reads(t):
+            la, lb = products[0, t], products[1, t]
+            squares = work.tile([P, 2 * S], F32, name="squares")
+            term1 = work.tile([P, S], F32, name="term1")
+            term2 = work.tile([P, S], F32, name="term2")
+            nc.scalar.activation(squares[:, :S], la[:], ACT.Square, scale=0.5**0.5)
+            nc.vector.tensor_tensor(term1[:], la[:], rows["u1", t][:], ALU.mult)
+            nc.scalar.activation(squares[:, S:], lb[:], ACT.Square)
+            nc.vector.tensor_tensor(term2[:], lb[:], rows["u2", t][:], ALU.mult)
+            return squares, term1, term2
 
-        def terms(t):
-            la, lb = banks[0, t], banks[1, t]
-            win = work.tile([P, 2 * S], F32, name="win")
-            a1 = work.tile([P, S], F32, name="a1")
-            a2 = work.tile([P, S], F32, name="a2")
-            nc.scalar.activation(win[:, :S], la[:], ACT.Square, scale=0.5**0.5)
-            nc.vector.tensor_tensor(a1[:], la[:], u1_sb[t][:], ALU.mult)
-            nc.scalar.activation(win[:, S:], lb[:], ACT.Square)
-            nc.vector.tensor_tensor(a2[:], lb[:], u2_sb[t][:], ALU.mult)
-            state[t] = (win, a1, a2)
-
-        def sums(t):
-            win, a1, a2 = state[t]
+        def sums(t, squares, term1, term2):
             own = work.tile([P, S], F32, name="own")
             grad = work.tile([P, S], F32, name="grad")
-            nc.vector.scalar_tensor_tensor(own[:], win[:, :S], 2.0, win[:, S:], ALU.mult, ALU.add)
-            if t in ALG_ON_PE:
-                alg = psum.tile([P, S], F32, name="turned", bufs=8 - FRONT)
-                turn(alg, (a1, a2))
-            else:
-                alg = work.tile([P, S], F32, name="alg")
-                nc.vector.tensor_tensor(alg[:], a1[:], a2[:], ALU.add)
-            if t in HM_ON_V:
-                nc.vector.tensor_tensor(grad[:], win[:].indirect(mod_sb[:]), own[:], ALU.add)
+            nc.vector.scalar_tensor_tensor(own[:], squares[:, :S], 2.0, squares[:, S:], ALU.mult, ALU.add)
+            alg_turned = transpose_and_add((term1, term2))
+            if t in PARTNER_ON_VECTOR:
+                nc.vector.tensor_tensor(grad[:], squares[:].indirect(mod_sb[:]), own[:], ALU.add)
             else:
                 partner = work.tile([P, S], F32, name="partner")
-                nc.scalar.activation(partner[:], win[:].indirect(mod_sb[:]), ACT.Copy)
+                nc.scalar.activation(partner[:], squares[:].indirect(mod_sb[:]), ACT.Copy)
                 nc.vector.tensor_tensor(grad[:], partner[:], own[:], ALU.add)
-            state[t] = (alg, grad)
+            return alg_turned, grad
 
-        def logs(t):
-            alg, grad = state[t]
-            alg2 = work.tile([P, S], F32, name="alg2")
-            log_alg = work.tile([P, S], F32, name="log_alg")
+        def logs(t, alg_turned, grad):
+            alg2_turned = work.tile([P, S], F32, name="alg2_turned")
+            log_alg2_turned = work.tile([P, S], F32, name="log_alg2_turned")
             log_num = work.tile([P, S], F32, name="log_num")
             num = work.tile([P, S], F32, name="num")
-            nc.scalar.activation(alg2[:], alg[:], ACT.Square)
-            nc.scalar.activation(log_alg[:], alg2[:], ACT.Ln, bias=2.0**-60)
-            if t in ALG_ON_PE:
-                back = psum.tile([P, S], F32, name="turned", bufs=8 - FRONT)
-                turn(back, (log_alg,))
-                log_alg = back
-            nc.vector.scalar_tensor_tensor(num[:], grad[:], 0.3, thr_sb[t][:], ALU.add, ALU.mult)
+            nc.scalar.activation(alg2_turned[:], alg_turned[:], ACT.Square)
+            nc.scalar.activation(log_alg2_turned[:], alg2_turned[:], ACT.Ln, bias=LOG_FLOOR)
+            log_alg2 = transpose_and_add((log_alg2_turned,))
+            nc.vector.scalar_tensor_tensor(num[:], grad[:], 0.3, rows["thr", t][:], ALU.add, ALU.mult)
             nc.scalar.activation(log_num[:], num[:], ACT.Ln)
-            state[t] = (log_num, log_alg)
+            return log_num, log_alg2
 
-        def log_odds(t):
-            log_num, log_alg = state[t]
-            nc.vector.tensor_tensor(odds[:, t, :], log_num[:], log_alg[:], ALU.subtract)
+        odds = keep.tile([P, PACK, S], F32, name="odds")
+        state = {}
+        for step in range(PACK + LOGS_LAG):
+            if step < PACK:
+                state[step] = first_reads(step)
+            if 0 <= step - SUMS_LAG < PACK:
+                state[step - SUMS_LAG] = sums(step - SUMS_LAG, *state[step - SUMS_LAG])
+            if 0 <= step - LOGS_LAG < PACK:
+                state[step - LOGS_LAG] = logs(step - LOGS_LAG, *state[step - LOGS_LAG])
+        for t in range(PACK):
+            log_num, log_alg2 = state[t]
+            nc.vector.tensor_tensor(odds[:, t, :], log_num[:], log_alg2[:], ALU.subtract)
 
-        stages = (products, terms, sums, logs, log_odds)
-        for step in range(PACK + max(LAG)):
-            for depth in ORDER:
-                t = step - LAG[depth]
-                if 0 <= t < PACK:
-                    stages[depth](t)
-
-        half = S // 2
         gm = keep.tile([P, PACK, S], F32, name="gm")
-        for c in range(2):
-            cols = slice(c * half, (c + 1) * half)
+        scaled_gm2 = keep.tile([P, PACK, S], F32, name="scaled_gm2")
+        halves = (slice(0, S // 2), slice(S // 2, S))
+        for cols in halves:
             nc.scalar.activation(gm[:, :, cols], odds[:, :, cols], ACT.Sigmoid)
-
-        square = keep.tile([P, PACK, S], F32, name="square")
-        for c in range(2):
-            cols = slice(c * half, (c + 1) * half)
+        for cols in halves:
             for t in range(PACK):
-                nc.vector.scalar_tensor_tensor(square[:, t, cols], gm[:, t, cols], unit_sb[:, t : t + 1], gm[:, t, cols], ALU.mult, ALU.mult)
+                nc.vector.scalar_tensor_tensor(
+                    scaled_gm2[:, t, cols], gm[:, t, cols], unit_sb[:, t : t + 1], gm[:, t, cols], ALU.mult, ALU.mult
+                )
 
-        start = 0
-        for width in CHUNKS:
-            cols = slice(start, start + width)
-            picks = mod_sb[:, start // 16 : (start + width) // 16]
-            start += width
-            planes = work.tile([P, PACK, width], BF16, name="planes", align_bytes=64)
+        for start in range(0, S, CHUNK):
+            cols = slice(start, start + CHUNK)
+            picks = mod_sb[:, start // PER_COLUMN : (start + CHUNK) // PER_COLUMN]
+
+            hid = work.tile([P, PACK, CHUNK], BF16, name="hid", align_bytes=64)
             for t in range(PACK):
-                wm = work.tile([P, width], F32, name="wm", bufs=8)
+                wm = work.tile([P, CHUNK], F32, name="wm", bufs=2 * PACK)
                 nc.scalar.activation(wm[:], gm[:, t, :].indirect(picks), ACT.Copy)
-                nc.vector.scalar_tensor_tensor(planes[:, t, :], wm[:], gain[:, t : t + 1], square[:, t, cols], ALU.mult, ALU.add)
-            grouped = work.tile([P, width, PACK], BF16, name="grouped", align_bytes=64)
-            codes = work.tile([P, width], U32, name="codes", align_bytes=64)
-            hscale = work.tile([P, width], U8, name="hscale", align_bytes=64)
+                nc.vector.scalar_tensor_tensor(
+                    hid[:, t, :], wm[:], half_unit[:, t : t + 1], scaled_gm2[:, t, cols], ALU.mult, ALU.add
+                )
+
+            grouped = work.tile([P, CHUNK, PACK], BF16, name="grouped", align_bytes=64)
+            codes = work.tile([P, CHUNK], U32, name="codes", align_bytes=64)
+            hid_scales = work.tile([P, CHUNK], U8, name="hid_scales", align_bytes=64)
             nc.vector.tensor_copy(
-                out=grouped[:].rearrange("p (c i) t -> p c t i", i=4),
-                in_=planes[:].rearrange("p t (c i) -> p c t i", i=4),
+                out=grouped[:].rearrange("p (c i) t -> p c t i", i=RUN),
+                in_=hid[:].rearrange("p t (c i) -> p c t i", i=RUN),
             )
-            nc.vector.quantize_mx(out=codes[:].bitcast(FP8X4), scales=hscale[:], in_=grouped[:].rearrange("p c t -> p (c t)"))
-            bank = psum.tile([P, 2, width], F32, name="bank", bufs=FRONT)
+            nc.vector.quantize_mx(out=codes[:].bitcast(FP8X4), scales=hid_scales[:], in_=grouped[:].rearrange("p c t -> p (c t)"))
+
+            mixed = psum.tile([P, N // P, CHUNK], F32, name="mixed", tag="bank")
             for m in range(N // P):
                 nc.tensor.matmul_mx(
-                    out=bank[:, m, :],
-                    lhsT=w3w[:, m * 2 * P : (m + 1) * 2 * P].bitcast(FP4X4),
+                    out=mixed[:, m, :],
+                    lhsT=w3w[:, m * FP4_BYTES * P : (m + 1) * FP4_BYTES * P].bitcast(FP4X4),
                     lhsT_scale=w3s[:, 0, m * P : (m + 1) * P],
                     rhs=codes[:].bitcast(FP8X4),
-                    rhs_scale=hscale[:],
+                    rhs_scale=hid_scales[:],
                     start=True,
                     stop=True,
                 )
-            res = work.tile([P, 2, width], F32, name="res")
-            nc.scalar.copy(res[:], bank[:])
-            nc.sync.dma_start(out=out[:, cols].rearrange("(m p) j -> p m j", p=P), in_=res[:])
+            result = work.tile([P, N // P, CHUNK], F32, name="result")
+            nc.scalar.copy(result[:], mixed[:])
+            nc.sync.dma_start(out=out[:, cols].rearrange("(m p) j -> p m j", p=P), in_=result[:])

@@ -25,6 +25,7 @@ FP4_BYTES = 2
 PER_COLUMN = 16
 BANKS = 8
 WORK_BUFS = PACK
+EARLY_TILES = PACK // 2
 CHUNK = 128
 RUN = 4
 
@@ -92,15 +93,13 @@ def tile_picked_ysampso_pair_p_kernel(
         load_scale_rows(ws_raw[0][:], w1_scales)
         load_x_words(1)
         load_scale_rows(ws_raw[1][:], w2_scales)
-        load_rows("u1", u1, 0)
-        load_rows("u2", u2, 0)
         nc.sync.dma_start(mod_sb[:], mod)
-        load_rows("thr", thr, 0)
-        nc.sync.dma_start(out=unit_sb[:], in_=unit.rearrange("(p t) o -> p (t o)", t=PACK))
-        for t in range(1, PACK):
+        for t in range(PACK):
             load_rows("u1", u1, t)
             load_rows("u2", u2, t)
+        for t in range(PACK):
             load_rows("thr", thr, t)
+        nc.sync.dma_start(out=unit_sb[:], in_=unit.rearrange("(p t) o -> p (t o)", t=PACK))
         nc.sync.dma_start(out=w3w[:].bitcast(I32), in_=w3_words[0].bitcast(I32))
         load_scale_rows(w3s[:], w3_scales)
 
@@ -115,14 +114,19 @@ def tile_picked_ysampso_pair_p_kernel(
             for t in range(count):
                 ww[n, first + t] = words[:, :, t, :]
 
-        def deal_scales(n):
-            ws[n] = keep.tile([P, PASSES, PACK, P], U8, name=f"ws{n}", align_bytes=64)
-            nc.gpsimd.tensor_copy(out=ws[n][:], in_=ws_raw[n][:].rearrange("p o (m t) -> p o t m", t=PACK))
+        def deal_scales(n, first, count, tag):
+            scales = keep.tile([P, PASSES, count, P], U8, name=f"ws{n}_{first}", tag=tag, align_bytes=64)
+            nc.gpsimd.tensor_copy(
+                out=scales[:], in_=ws_raw[n][:].rearrange("p o (m t) -> p o t m", t=PACK)[:, :, first : first + count]
+            )
+            for t in range(count):
+                ws[n, first + t] = scales[:, :, t, :]
 
         deal_words(nc.gpsimd, 0, 0, PACK, "ww0")
-        deal_scales(0)
-        deal_words(nc.gpsimd, 1, 0, 1, "ws_raw0")
-        deal_scales(1)
+        deal_words(nc.gpsimd, 1, 0, EARLY_TILES, "ww1")
+        deal_scales(0, 0, EARLY_TILES, "ws0")
+        deal_scales(1, 0, PACK, "ws1")
+        deal_scales(0, EARLY_TILES, PACK - EARLY_TILES, "ws_raw1")
 
         xs, xw = [], []
         for o in range(PASSES):
@@ -134,7 +138,7 @@ def tile_picked_ysampso_pair_p_kernel(
             nc.vector.tensor_copy(picked_words[:], xw_raw[o][:].indirect(offs_sb[:]))
             xw.append(picked_words)
 
-        deal_words(nc.vector, 1, 1, PACK - 1, f"xw_raw{PASSES - 1}")
+        deal_words(nc.vector, 1, EARLY_TILES, PACK - EARLY_TILES, f"xw_raw{PASSES - 1}")
 
         half_unit = keep.tile([P, PACK], F32, name="half_unit")
         nc.vector.tensor_scalar(half_unit[:], unit_sb[:], -0.5, None, ALU.mult)
@@ -147,7 +151,7 @@ def tile_picked_ysampso_pair_p_kernel(
                     nc.tensor.matmul_mx(
                         out=products[n, t][:],
                         lhsT=ww[n, t][:, o, :].bitcast(FP4X4),
-                        lhsT_scale=ws[n][:, o, t, :],
+                        lhsT_scale=ws[n, t][:, o, :],
                         rhs=xw[o][:].bitcast(FP8X4),
                         rhs_scale=xs[o][:],
                         start=(o == 0),

from contextlib import ExitStack

import concourse.mybir as mybir
from concourse.masks import make_identity

K, T, S, N, H = 1024, 1024, 512, 256, 512
FLOPS = 2 * (2 * K * H * S + H * N * S)

F32 = mybir.dt.float32
BF16 = mybir.dt.bfloat16
I32 = mybir.dt.int32
U32 = mybir.dt.uint32
U16 = mybir.dt.uint16
U8 = mybir.dt.uint8
FP8X4 = mybir.dt.float8_e4m3fn_x4
FP4X4 = mybir.dt.float4_e2m1fn_x4
ACT = mybir.ActivationFunctionType
ALU = mybir.AluOpType

P = 128
PACK = 4
PASSES = K // (P * PACK)
QUADRANTS = 4
FP4_BYTES = 2
PER_COLUMN = 16
BANKS = 8
WORK_BUFS = PACK
EARLY_TILES = PACK // 2
CHUNK = 128
RUN = 4

LOG_FLOOR = 2.0**-60

PARTNER_ON_VECTOR = (0, 3)

SUMS_LAG, LOGS_LAG = 1, 3


def tile_picked_ysampso_pair_p_kernel(
    tc, x_words, x_scales, w1_words, w1_scales, w2_words, w2_scales, u1, u2, thr, unit, w3_words, w3_scales, offs, mod, out
):
    nc = tc.nc
    with ExitStack() as ctx:
        keep = ctx.enter_context(tc.tile_pool(name="keep", bufs=1))
        work = ctx.enter_context(tc.tile_pool(name="work", bufs=WORK_BUFS))
        psum = ctx.enter_context(tc.psum_pool(name="psum", bufs=BANKS))

        offs_sb = keep.tile([P, S // PER_COLUMN], U16, name="offs_sb")
        mod_sb = keep.tile([P, S // PER_COLUMN], U16, name="mod_sb")
        xs_raw = keep.tile([P, PASSES, T], U8, name="xs_raw", align_bytes=64)
        ws_raw = [keep.tile([P, PASSES, H], U8, name=f"ws_raw{n}", align_bytes=64) for n in range(2)]
        w3s = keep.tile([P, 1, N], U8, name="w3s", align_bytes=64)
        ww_raw = [keep.tile([P, PASSES, FP4_BYTES * H], U8, name=f"ww_raw{n}", align_bytes=64) for n in range(2)]
        w3w = keep.tile([P, FP4_BYTES * N], U8, name="w3w", align_bytes=64)
        xw_raw = [keep.tile([P, T], U32, name=f"xw_raw{o}", align_bytes=64) for o in range(PASSES)]
        ident = keep.tile([P, P], F32, name="ident")
        unit_sb = keep.tile([P, PACK], F32, name="unit_sb")

        nc.gpsimd.memset(xs_raw[:].bitcast(I32), 0)
        for n in range(2):
            nc.vector.memset(ws_raw[n][:].bitcast(I32), 0)
        nc.vector.memset(w3s[:].bitcast(I32), 0)
        make_identity(nc, ident[:])

        warm = keep.tile([P, 2], F32, name="warm")
        nc.vector.memset(warm[:, 0:1], 1.0)
        nc.scalar.activation(warm[:, 1:2], warm[:, 0:1], ACT.Ln)

        def load_scale_rows(dst, src):
            for q in range(QUADRANTS):
                nc.sync.dma_start(
                    out=dst[32 * q : 32 * q + 4].bitcast(I32),
                    in_=src[:, 4 * q : 4 * q + 4, :].rearrange("o r c -> r o c").bitcast(I32),
                )

        def load_w_words(n, src):
            nc.sync.dma_start(out=ww_raw[n][:].bitcast(I32), in_=src.rearrange("o p c -> p o c").bitcast(I32))

        def load_x_words(o):
            nc.sync.dma_start(out=xw_raw[o][:].bitcast(I32), in_=x_words[o].rearrange("p n t -> p (n t)").bitcast(I32))

        rows = {}

        def load_rows(name, src, t):
            rows[name, t] = keep.tile([P, S], F32, name=f"{name}_{t}")
            nc.sync.dma_start(out=rows[name, t][:], in_=src.rearrange("(p t) j -> t p j", t=PACK)[t])

        load_w_words(0, w1_words)
        nc.sync.dma_start(offs_sb[:], offs)
        load_scale_rows(xs_raw[:], x_scales)
        load_x_words(0)
        load_w_words(1, w2_words)
        load_scale_rows(ws_raw[0][:], w1_scales)
        load_x_words(1)
        load_scale_rows(ws_raw[1][:], w2_scales)
        nc.sync.dma_start(mod_sb[:], mod)
        for t in range(PACK):
            load_rows("u1", u1, t)
            load_rows("u2", u2, t)
        for t in range(PACK):
            load_rows("thr", thr, t)
        nc.sync.dma_start(out=unit_sb[:], in_=unit.rearrange("(p t) o -> p (t o)", t=PACK))
        nc.sync.dma_start(out=w3w[:].bitcast(I32), in_=w3_words[0].bitcast(I32))
        load_scale_rows(w3s[:], w3_scales)

        ww, ws = {}, {}

        def deal_words(engine, n, first, count, tag):
            words = keep.tile([P, PASSES, count, FP4_BYTES * P], U8, name=f"ww{n}_{first}", tag=tag, align_bytes=64)
            engine.tensor_copy(
                out=words[:].rearrange("p o t (m b) -> p o t m b", b=FP4_BYTES),
                in_=ww_raw[n][:].rearrange("p o (m t b) -> p o t m b", t=PACK, b=FP4_BYTES)[:, :, first : first + count],
            )
            for t in range(count):
                ww[n, first + t] = words[:, :, t, :]

        def deal_scales(n, first, count, tag):
            scales = keep.tile([P, PASSES, count, P], U8, name=f"ws{n}_{first}", tag=tag, align_bytes=64)
            nc.gpsimd.tensor_copy(
                out=scales[:], in_=ws_raw[n][:].rearrange("p o (m t) -> p o t m", t=PACK)[:, :, first : first + count]
            )
            for t in range(count):
                ws[n, first + t] = scales[:, :, t, :]

        deal_words(nc.gpsimd, 0, 0, PACK, "ww0")
        deal_words(nc.gpsimd, 1, 0, EARLY_TILES, "ww1")
        deal_scales(0, 0, EARLY_TILES, "ws0")
        deal_scales(1, 0, PACK, "ws1")
        deal_scales(0, EARLY_TILES, PACK - EARLY_TILES, "ws_raw1")

        xs, xw = [], []
        for o in range(PASSES):
            picked_scales = keep.tile([P, S], U8, name=f"xs{o}", align_bytes=64)
            nc.vector.tensor_copy(picked_scales[:], xs_raw[:, o, :].indirect(offs_sb[:]))
            xs.append(picked_scales)
        for o in range(PASSES):
            picked_words = keep.tile([P, S], U32, name=f"xw{o}", align_bytes=64)
            nc.vector.tensor_copy(picked_words[:], xw_raw[o][:].indirect(offs_sb[:]))
            xw.append(picked_words)

        deal_words(nc.vector, 1, EARLY_TILES, PACK - EARLY_TILES, f"xw_raw{PASSES - 1}")

        half_unit = keep.tile([P, PACK], F32, name="half_unit")
        nc.vector.tensor_scalar(half_unit[:], unit_sb[:], -0.5, None, ALU.mult)

        products = {}
        for t in range(PACK):
            for n in range(2):
                products[n, t] = psum.tile([P, S], F32, name="product", tag="bank")
                for o in range(PASSES):
                    nc.tensor.matmul_mx(
                        out=products[n, t][:],
                        lhsT=ww[n, t][:, o, :].bitcast(FP4X4),
                        lhsT_scale=ws[n, t][:, o, :],
                        rhs=xw[o][:].bitcast(FP8X4),
                        rhs_scale=xs[o][:],
                        start=(o == 0),
                        stop=(o == PASSES - 1),
                    )

        def transpose_and_add(parts):
            bank = psum.tile([P, S], F32, name="turned", tag="bank")
            for b in range(0, S, P):
                for n, part in enumerate(parts):
                    nc.tensor.matmul(
                        bank[:, b : b + P],
                        part[:, b : b + P],
                        ident[:],
                        start=(n == 0),
                        stop=(n == len(parts) - 1),
                        is_transpose=True,
                    )
            return bank

        def first_reads(t):
            la, lb = products[0, t], products[1, t]
            squares = work.tile([P, 2 * S], F32, name="squares")
            term1 = work.tile([P, S], F32, name="term1")
            term2 = work.tile([P, S], F32, name="term2")
            nc.scalar.activation(squares[:, :S], la[:], ACT.Square, scale=0.5**0.5)
            nc.vector.tensor_tensor(term1[:], la[:], rows["u1", t][:], ALU.mult)
            nc.scalar.activation(squares[:, S:], lb[:], ACT.Square)
            nc.vector.tensor_tensor(term2[:], lb[:], rows["u2", t][:], ALU.mult)
            return squares, term1, term2

        def sums(t, squares, term1, term2):
            own = work.tile([P, S], F32, name="own")
            grad = work.tile([P, S], F32, name="grad")
            nc.vector.scalar_tensor_tensor(own[:], squares[:, :S], 2.0, squares[:, S:], ALU.mult, ALU.add)
            alg_turned = transpose_and_add((term1, term2))
            if t in PARTNER_ON_VECTOR:
                nc.vector.tensor_tensor(grad[:], squares[:].indirect(mod_sb[:]), own[:], ALU.add)
            else:
                partner = work.tile([P, S], F32, name="partner")
                nc.scalar.activation(partner[:], squares[:].indirect(mod_sb[:]), ACT.Copy)
                nc.vector.tensor_tensor(grad[:], partner[:], own[:], ALU.add)
            return alg_turned, grad

        def logs(t, alg_turned, grad):
            alg2_turned = work.tile([P, S], F32, name="alg2_turned")
            log_alg2_turned = work.tile([P, S], F32, name="log_alg2_turned")
            log_num = work.tile([P, S], F32, name="log_num")
            num = work.tile([P, S], F32, name="num")
            nc.scalar.activation(alg2_turned[:], alg_turned[:], ACT.Square)
            nc.scalar.activation(log_alg2_turned[:], alg2_turned[:], ACT.Ln, bias=LOG_FLOOR)
            log_alg2 = transpose_and_add((log_alg2_turned,))
            nc.vector.scalar_tensor_tensor(num[:], grad[:], 0.3, rows["thr", t][:], ALU.add, ALU.mult)
            nc.scalar.activation(log_num[:], num[:], ACT.Ln)
            return log_num, log_alg2

        odds = keep.tile([P, PACK, S], F32, name="odds")
        state = {}
        for step in range(PACK + LOGS_LAG):
            if step < PACK:
                state[step] = first_reads(step)
            if 0 <= step - SUMS_LAG < PACK:
                state[step - SUMS_LAG] = sums(step - SUMS_LAG, *state[step - SUMS_LAG])
            if 0 <= step - LOGS_LAG < PACK:
                state[step - LOGS_LAG] = logs(step - LOGS_LAG, *state[step - LOGS_LAG])
        for t in range(PACK):
            log_num, log_alg2 = state[t]
            nc.vector.tensor_tensor(odds[:, t, :], log_num[:], log_alg2[:], ALU.subtract)

        gm = keep.tile([P, PACK, S], F32, name="gm")
        scaled_gm2 = keep.tile([P, PACK, S], F32, name="scaled_gm2")
        halves = (slice(0, S // 2), slice(S // 2, S))
        for cols in halves:
            nc.scalar.activation(gm[:, :, cols], odds[:, :, cols], ACT.Sigmoid)
        for cols in halves:
            for t in range(PACK):
                nc.vector.scalar_tensor_tensor(
                    scaled_gm2[:, t, cols], gm[:, t, cols], unit_sb[:, t : t + 1], gm[:, t, cols], ALU.mult, ALU.mult
                )

        for start in range(0, S, CHUNK):
            cols = slice(start, start + CHUNK)
            picks = mod_sb[:, start // PER_COLUMN : (start + CHUNK) // PER_COLUMN]

            hid = work.tile([P, PACK, CHUNK], BF16, name="hid", align_bytes=64)
            for t in range(PACK):
                wm = work.tile([P, CHUNK], F32, name="wm", bufs=2 * PACK)
                nc.scalar.activation(wm[:], gm[:, t, :].indirect(picks), ACT.Copy)
                nc.vector.scalar_tensor_tensor(
                    hid[:, t, :], wm[:], half_unit[:, t : t + 1], scaled_gm2[:, t, cols], ALU.mult, ALU.add
                )

            grouped = work.tile([P, CHUNK, PACK], BF16, name="grouped", align_bytes=64)
            codes = work.tile([P, CHUNK], U32, name="codes", align_bytes=64)
            hid_scales = work.tile([P, CHUNK], U8, name="hid_scales", align_bytes=64)
            nc.vector.tensor_copy(
                out=grouped[:].rearrange("p (c i) t -> p c t i", i=RUN),
                in_=hid[:].rearrange("p t (c i) -> p c t i", i=RUN),
            )
            nc.vector.quantize_mx(out=codes[:].bitcast(FP8X4), scales=hid_scales[:], in_=grouped[:].rearrange("p c t -> p (c t)"))

            mixed = psum.tile([P, N // P, CHUNK], F32, name="mixed", tag="bank")
            for m in range(N // P):
                nc.tensor.matmul_mx(
                    out=mixed[:, m, :],
                    lhsT=w3w[:, m * FP4_BYTES * P : (m + 1) * FP4_BYTES * P].bitcast(FP4X4),
                    lhsT_scale=w3s[:, 0, m * P : (m + 1) * P],
                    rhs=codes[:].bitcast(FP8X4),
                    rhs_scale=hid_scales[:],
                    start=True,
                    stop=True,
                )
            result = work.tile([P, N // P, CHUNK], F32, name="result")
            nc.scalar.copy(result[:], mixed[:])
            nc.sync.dma_start(out=out[:, cols].rearrange("(m p) j -> p m j", p=P), in_=result[:])
